import numpy as np
import ml_dtypes


def mxq(x, axis, fmt="e4m3"):
    dtype, down = {"e4m3": (ml_dtypes.float8_e4m3fn, 7), "e5m2": (ml_dtypes.float8_e5m2, 14)}[fmt]
    v = np.moveaxis(np.asarray(x, np.float32).astype(ml_dtypes.bfloat16).astype(np.float64), axis, -1)
    blocks = v.reshape(v.shape[:-1] + (-1, 32))
    amax = np.abs(blocks).max(-1, keepdims=True)
    byte = np.maximum(np.where(amax > 0, np.frexp(amax)[1] - 1 + 127, 0) - down, 1)
    scale = np.exp2(byte - 127.0)
    codes = (blocks / scale).astype(np.float32).astype(dtype).astype(np.float64)
    return np.moveaxis((codes * scale).reshape(v.shape), -1, axis)


WIDE = False


def mx_kscale(k):
    if not WIDE:
        return np.ones(k)
    levels = np.array([10, -10, 5, -5, 0])
    if k % 512:
        return np.exp2(np.random.permutation(np.resize(levels, k // 32))).repeat(32)
    a = np.empty((k // 512, 16))
    for p in range(k // 512):
        a[p, :8] = np.random.permutation(np.resize(levels, 8))
        for g in range(8):
            far = levels[np.abs(levels - a[p, g]) >= 10]
            a[p, g + 8] = far[np.random.randint(len(far))]
    return np.exp2(a.ravel()).repeat(32)


def f64(x):
    return np.asarray(x).astype(np.float64)


def striped(idx):
    return np.tile(idx.reshape(-1, 16).T, (8, 1)).astype(np.uint16)


def unstriped(offs):
    return offs[:16].T.reshape(-1).astype(np.int64)


def pack_weight(w):
    k, n = w.shape
    w = f64(np.asarray(w, np.float32).astype(ml_dtypes.bfloat16)).reshape(k // 32, 32, n)
    amax = np.abs(w).max(1)
    byte = np.clip(np.where(amax > 0, np.frexp(amax)[1] - 1 + 127 - 7, 1), 1, 254)
    scaled = (w * np.exp2(127.0 - byte)[:, None, :]).reshape(k, n).astype(np.float32)
    words = np.ascontiguousarray(scaled.reshape(k // 512, 128, 4, n).transpose(0, 1, 3, 2)).astype(ml_dtypes.float8_e4m3fn).view(np.uint8)
    return words, np.ascontiguousarray(byte.astype(np.uint8).reshape(k // 512, 16, n))


def unpack_weight(words, scales):
    g, p, n, _ = words.shape
    vals = np.ascontiguousarray(words).view(ml_dtypes.float8_e4m3fn).astype(np.float64) * np.repeat(np.exp2(scales.astype(np.float64) - 127.0), 8, axis=1)[..., None]
    return vals.transpose(0, 1, 3, 2).reshape(g * 512, n)


def relu(v):
    return np.maximum(v, 0.0)


K, T, S, N, U = 1024, 1024, 512, 256, 1024


def setup_inputs():
    n = np.random.standard_normal
    s = mx_kscale(K)[:, None]
    packed_xT = pack_weight(n((K, T)) * s)
    return {
        "x_words": packed_xT[0],
        "x_scales": packed_xT[1],
        "w1": (n((K, N)) / np.sqrt(K) / s).astype(np.float32),
        "var": (np.random.uniform(0.3, 2.0, (N, U))).astype(np.float32),
        "omega": (np.random.uniform(0.02, 0.15, (N, 1))).astype(np.float32),
        "offs": striped(np.random.permutation(T)[:S]),
        "ser": striped(np.random.permutation(U)[:S]),
    }


def reference(x_words, x_scales, w1, var, omega, offs, ser):
    v0 = f64(var)[:, unstriped(ser)]
    xq = unpack_weight(x_words, x_scales)[:, unstriped(offs)]
    y = mxq(f64(w1), 0, "e4m3").T @ xq
    shk = (0.9 * y) * np.sqrt(v0)
    v1 = 0.8 * v0 + f64(omega) + 0.08 * ((shk) ** 2) + 0.12 * ((relu(-1.0 * shk)) ** 2)
    out = f64(var).copy()
    out[:, unstriped(ser)] = v1
    return out

@@ -1,0 +1,167 @@
+import math
+from contextlib import ExitStack
+
+import concourse.mybir as mybir
+from concourse.masks import make_identity
+
+K, T, S, N, U = 1024, 1024, 512, 256, 1024
+FLOPS = 2 * K * N * S
+
+F32 = mybir.dt.float32
+BF16 = mybir.dt.bfloat16
+I32 = mybir.dt.int32
+U32 = mybir.dt.uint32
+U16 = mybir.dt.uint16
+U8 = mybir.dt.uint8
+FP8X4 = mybir.dt.float8_e4m3fn_x4
+ACT = mybir.ActivationFunctionType
+ALU = mybir.AluOpType
+
+P = 128
+PACK = 4
+K_PASS = P * PACK
+PASSES = K // K_PASS
+BLOCKS = N // P
+LIST_COL = 16
+ROOT_SYM = 0.9 * math.sqrt(0.08)
+ROOT_NEG = 0.9 * math.sqrt(0.12)
+KEEP = 0.8
+
+
+def tile_picked_ygjrg_put_p_kernel(tc, x_words, x_scales, w1, var, omega, offs, ser, out):
+    nc = tc.nc
+    with ExitStack() as ctx:
+        held = ctx.enter_context(tc.tile_pool(name="held", bufs=1))
+        psum = ctx.enter_context(tc.psum_pool(name="psum", bufs=1))
+
+        offs_sb = held.tile([P, S // LIST_COL], U16, name="offs_sb")
+        ser_sb = held.tile([P, S // LIST_COL], U16, name="ser_sb")
+        scale_tab = held.tile([P, T], U8, name="scale_tab", align_bytes=64)
+        word_tab = [held.tile([P, T], U32, name=f"word_tab{g}", tag=f"table{g}", align_bytes=64) for g in range(PASSES)]
+        w_raw = {}
+        var_sb = {}
+        omega_sb = held.tile([P, BLOCKS], F32, name="omega_sb")
+        ident = held.tile([P, P], F32, name="ident", align_bytes=64)
+
+        def load_w(b):
+            for g in range(PASSES):
+                w_raw[b, g] = held.tile([P, PACK, P], F32, name=f"w_raw{b}{g}", tag=f"w_raw{g}", align_bytes=64)
+                rows = w1[g * K_PASS : (g + 1) * K_PASS, b * P : (b + 1) * P]
+                nc.sync.dma_start(w_raw[b, g][:], rows.rearrange("(p j) c -> p j c", j=PACK))
+
+        def load_var(b):
+            var_sb[b] = held.tile([P, U], F32, name=f"var_sb{b}", tag=f"table{b}", align_bytes=64)
+            nc.sync.dma_start(var_sb[b][:], var[b * P : (b + 1) * P, :])
+
+        def load_words(g):
+            nc.sync.dma_start(word_tab[g][:].bitcast(I32), x_words[g].rearrange("p n t -> p (n t)").bitcast(I32))
+
+        nc.gpsimd.memset(scale_tab[:].bitcast(I32), 0)
+        nc.sync.dma_start(offs_sb[:], offs)
+        for q in range(4):
+            nc.scalar.dma_start(scale_tab[32 * q : 32 * q + 4 * PASSES, :].bitcast(I32), x_scales[:, 4 * q : 4 * q + 4, :].bitcast(I32))
+        load_words(0)
+        load_w(0)
+        load_words(1)
+        nc.sync.dma_start(ser_sb[:], ser)
+        with nc.allow_non_contiguous_dma(reason="one constant a row"):
+            nc.gpsimd.dma_start(omega_sb[:], omega.rearrange("(b p) o -> p (b o)", p=P))
+        make_identity(nc, ident[:])
+
+        omega_wide = [held.tile([P, S // 2], F32, name=f"omega_wide{b}", align_bytes=64) for b in range(BLOCKS)]
+
+        x_scale = held.tile([P, S], U8, name="x_scale", align_bytes=64)
+        x_code = [held.tile([P, S], U32, name=f"x_code{g}", align_bytes=64) for g in range(PASSES)]
+        w_code = {}
+        w_scale = [held.tile([P, PASSES, P], U8, name=f"w_scale{b}", align_bytes=64) for b in range(BLOCKS)]
+        w_bf = {}
+        v0 = {}
+
+        def entries(lst, lo, hi):
+            return lst[:, lo // LIST_COL : hi // LIST_COL]
+
+        def cast_w(b, g, tag):
+            if g == 0:
+                w_bf[b] = held.tile([P, PASSES, P, PACK], BF16, name=f"w_bf{b}", tag=tag, align_bytes=64)
+            nc.scalar.copy(
+                w_bf[b][:, g].rearrange("p (c i) t -> p c t i", i=4),
+                w_raw[b, g][:].rearrange("p t (c i) -> p c t i", i=4),
+            )
+
+        def quantise_w(b, g0, g1, tag):
+            if g0 == 0:
+                w_code[b] = held.tile([P, PASSES, P], U32, name=f"w_code{b}", tag=tag, align_bytes=64)
+            nc.vector.quantize_mx(
+                out=w_code[b][:, g0:g1].rearrange("p g c -> p (g c)").bitcast(FP8X4),
+                scales=w_scale[b][:, g0:g1].rearrange("p g c -> p (g c)"),
+                in_=w_bf[b][:, g0:g1].rearrange("p g c t -> p (g c t)"),
+            )
+
+        def gather_words(g, lo, hi):
+            nc.vector.tensor_copy(x_code[g][:, lo:hi], word_tab[g][:].indirect(entries(offs_sb, lo, hi)))
+
+        def growth(b, lo, hi, neg_tag):
+            n = (hi - lo) // P
+            y_t = psum.tile([P, n, P], F32, name=f"y_t{b}_{lo}")
+            for i in range(n):
+                cols = slice(lo + i * P, lo + (i + 1) * P)
+                for g in range(PASSES):
+                    nc.tensor.matmul_mx(
+                        out=y_t[:, i],
+                        lhsT=x_code[g][:, cols].bitcast(FP8X4),
+                        lhsT_scale=x_scale[4 * g :, cols],
+                        rhs=w_code[b][:, g].bitcast(FP8X4),
+                        rhs_scale=w_scale[b][:, g],
+                        start=(g == 0),
+                        stop=(g == PASSES - 1),
+                    )
+            neg = held.tile([P, n, P], F32, name=f"neg{b}_{lo}", tag=neg_tag, align_bytes=64)
+            neg_sq = held.tile([P, n, P], F32, name=f"neg_sq{b}_{lo}", align_bytes=64)
+            sym_sq = held.tile([P, n, P], F32, name=f"sym_sq{b}_{lo}", align_bytes=64)
+            nc.scalar.activation(neg[:], y_t[:], ACT.Relu, scale=-ROOT_NEG)
+            nc.scalar.activation(sym_sq[:], y_t[:], ACT.Square, scale=ROOT_SYM)
+            nc.scalar.activation(neg_sq[:], neg[:], ACT.Square)
+            acc = psum.tile([P, n * P], F32, name=f"acc{b}_{lo}")
+            for i in range(n):
+                dst = acc[:, i * P : (i + 1) * P]
+                nc.tensor.matmul(dst, sym_sq[:, i], ident[:], start=True, stop=False, is_transpose=True)
+                nc.tensor.matmul(dst, neg_sq[:, i], ident[:], start=False, stop=True, is_transpose=True)
+            return acc
+
+        def put_back(b, lo, hi, acc, tag):
+            scaled = held.tile([P, hi - lo], F32, name=f"scaled{b}_{lo}", tag=tag, align_bytes=64)
+            nc.vector.scalar_tensor_tensor(scaled[:], acc[:], KEEP, v0[b][:, lo:hi], ALU.add, ALU.mult)
+            nc.vector.tensor_tensor(var_sb[b][:].indirect(entries(ser_sb, lo, hi)), scaled[:], omega_wide[b][:], ALU.add)
+
+        def gather_var(b, tag):
+            v0[b] = held.tile([P, S], F32, name=f"v0_{b}", tag=tag, align_bytes=64)
+            nc.vector.tensor_copy(v0[b][:], var_sb[b][:].indirect(ser_sb[:]))
+
+        half = S // 2
+        nc.vector.tensor_copy(x_scale[:], scale_tab[:].indirect(offs_sb[:]))
+        gather_words(0, 0, S)
+        load_var(0)
+        for g in range(PASSES):
+            cast_w(0, g, "w_bf0")
+            quantise_w(0, g, g + 1, "w_code0")
+        load_w(1)
+        for b in range(BLOCKS):
+            nc.scalar.copy(omega_wide[b][:], omega_sb[:, b : b + 1].to_broadcast([P, S // 2]))
+        gather_words(1, 0, half)
+        gather_words(1, half, S)
+        load_var(1)
+        acc_a = growth(0, 0, half, "chain")
+        acc_b = growth(0, half, S, "neg_b")
+        gather_var(0, "v0_0")
+        for g in range(PASSES):
+            cast_w(1, g, "chain")
+        put_back(0, 0, half, acc_a, "first")
+        quantise_w(1, 0, PASSES, "first")
+        acc_c = growth(1, 0, half, "neg_c")
+        acc_d = growth(1, half, S, "neg_d")
+        put_back(0, half, S, acc_b, "chain")
+        nc.sync.dma_start(out[0:P, :], var_sb[0][:])
+        gather_var(1, "chain")
+        put_back(1, 0, half, acc_c, "scaled_c")
+        put_back(1, half, S, acc_d, "scaled_d")
+        nc.sync.dma_start(out[P : 2 * P, :], var_sb[1][:])

@@ -33,24 +33,20 @@ def tile_picked_ygjrg_put_p_kernel(tc, x_words, x_scales, w1, var, omega, offs, 
     with ExitStack() as ctx:
         held = ctx.enter_context(tc.tile_pool(name="held", bufs=1))
         psum = ctx.enter_context(tc.psum_pool(name="psum", bufs=1))
+        half = S // 2
 
         offs_sb = held.tile([P, S // LIST_COL], U16, name="offs_sb")
         ser_sb = held.tile([P, S // LIST_COL], U16, name="ser_sb")
         scale_tab = held.tile([P, T], U8, name="scale_tab", align_bytes=64)
-        word_tab = [held.tile([P, T], U32, name=f"word_tab{g}", tag=f"table{g}", align_bytes=64) for g in range(PASSES)]
-        w_raw = {}
-        var_sb = {}
+        scale_rows = held.tile([P, T // 4], I32, name="scale_rows", align_bytes=64)
+        word_tab = [held.tile([P, T], U32, name=f"word_tab{g}", align_bytes=64) for g in range(PASSES)]
+        w_raw = [held.tile([P, PACK, N], F32, name=f"w_raw{g}", align_bytes=64) for g in range(PASSES)]
         omega_sb = held.tile([P, BLOCKS], F32, name="omega_sb")
         ident = held.tile([P, P], F32, name="ident", align_bytes=64)
-
-        def load_w(b):
-            for g in range(PASSES):
-                w_raw[b, g] = held.tile([P, PACK, P], F32, name=f"w_raw{b}{g}", tag=f"w_raw{g}", align_bytes=64)
-                rows = w1[g * K_PASS : (g + 1) * K_PASS, b * P : (b + 1) * P]
-                nc.sync.dma_start(w_raw[b, g][:], rows.rearrange("(p j) c -> p j c", j=PACK))
+        var_sb = {}
 
         def load_var(b):
-            var_sb[b] = held.tile([P, U], F32, name=f"var_sb{b}", tag=f"table{b}", align_bytes=64)
+            var_sb[b] = held.tile([P, U], F32, name=f"var_sb{b}", align_bytes=64)
             nc.sync.dma_start(var_sb[b][:], var[b * P : (b + 1) * P, :])
 
         def load_words(g):
@@ -59,48 +55,48 @@ def tile_picked_ygjrg_put_p_kernel(tc, x_words, x_scales, w1, var, omega, offs, 
         nc.gpsimd.memset(scale_tab[:].bitcast(I32), 0)
         nc.sync.dma_start(offs_sb[:], offs)
         for q in range(4):
-            nc.scalar.dma_start(scale_tab[32 * q : 32 * q + 4 * PASSES, :].bitcast(I32), x_scales[:, 4 * q : 4 * q + 4, :].bitcast(I32))
-        load_words(0)
-        load_w(0)
-        load_words(1)
-        nc.sync.dma_start(ser_sb[:], ser)
+            nc.sync.dma_start(scale_rows[32 * q : 32 * q + 4 * PASSES, :], x_scales[:, 4 * q : 4 * q + 4, :].bitcast(I32))
         with nc.allow_non_contiguous_dma(reason="one constant a row"):
-            nc.gpsimd.dma_start(omega_sb[:], omega.rearrange("(b p) o -> p (b o)", p=P))
+            nc.sync.dma_start(omega_sb[:], omega.rearrange("(b p) o -> p (b o)", p=P))
+        load_words(0)
+        load_words(1)
+        for g in range(PASSES):
+            nc.sync.dma_start(w_raw[g][:], w1[g * K_PASS : (g + 1) * K_PASS, :].rearrange("(p j) c -> p j c", j=PACK))
+        nc.sync.dma_start(ser_sb[:], ser)
+        load_var(0)
+        load_var(1)
         make_identity(nc, ident[:])
 
-        omega_wide = [held.tile([P, S // 2], F32, name=f"omega_wide{b}", align_bytes=64) for b in range(BLOCKS)]
-
+        omega_wide = [held.tile([P, (half, S)[b]], F32, name=f"omega_wide{b}", align_bytes=64) for b in range(BLOCKS)]
         x_scale = held.tile([P, S], U8, name="x_scale", align_bytes=64)
         x_code = [held.tile([P, S], U32, name=f"x_code{g}", align_bytes=64) for g in range(PASSES)]
-        w_code = {}
-        w_scale = [held.tile([P, PASSES, P], U8, name=f"w_scale{b}", align_bytes=64) for b in range(BLOCKS)]
-        w_bf = {}
-        v0 = {}
+        w_code = [held.tile([P, N], U32, name=f"w_code{g}", align_bytes=64) for g in range(PASSES)]
+        w_scale = [held.tile([P, N], U8, name=f"w_scale{g}", align_bytes=64) for g in range(PASSES)]
+        w_bf = [held.tile([P, N, PACK], BF16, name=f"w_bf{g}", align_bytes=64) for g in range(PASSES)]
+        v0 = held.tile([P, BLOCKS, S], F32, name="v0", align_bytes=64)
+        scaled = [held.tile([P, S], F32, name=f"scaled{b}", align_bytes=64) for b in range(BLOCKS)]
 
         def entries(lst, lo, hi):
             return lst[:, lo // LIST_COL : hi // LIST_COL]
 
-        def cast_w(b, g, tag):
-            if g == 0:
-                w_bf[b] = held.tile([P, PASSES, P, PACK], BF16, name=f"w_bf{b}", tag=tag, align_bytes=64)
+        def quantise_w(g, lo, hi):
             nc.scalar.copy(
-                w_bf[b][:, g].rearrange("p (c i) t -> p c t i", i=4),
-                w_raw[b, g][:].rearrange("p t (c i) -> p c t i", i=4),
+                w_bf[g][:, lo:hi].rearrange("p (c i) t -> p c t i", i=4),
+                w_raw[g][:, :, lo:hi].rearrange("p t (c i) -> p c t i", i=4),
             )
-
-        def quantise_w(b, g0, g1, tag):
-            if g0 == 0:
-                w_code[b] = held.tile([P, PASSES, P], U32, name=f"w_code{b}", tag=tag, align_bytes=64)
             nc.vector.quantize_mx(
-                out=w_code[b][:, g0:g1].rearrange("p g c -> p (g c)").bitcast(FP8X4),
-                scales=w_scale[b][:, g0:g1].rearrange("p g c -> p (g c)"),
-                in_=w_bf[b][:, g0:g1].rearrange("p g c t -> p (g c t)"),
+                out=w_code[g][:, lo:hi].bitcast(FP8X4),
+                scales=w_scale[g][:, lo:hi],
+                in_=w_bf[g][:, lo:hi].rearrange("p c t -> p (c t)"),
             )
 
         def gather_words(g, lo, hi):
             nc.vector.tensor_copy(x_code[g][:, lo:hi], word_tab[g][:].indirect(entries(offs_sb, lo, hi)))
 
-        def growth(b, lo, hi, neg_tag):
+        def gather_var(b):
+            nc.vector.tensor_copy(v0[:, b], var_sb[b][:].indirect(ser_sb[:]))
+
+        def growth(b, lo, hi):
             n = (hi - lo) // P
             y_t = psum.tile([P, n, P], F32, name=f"y_t{b}_{lo}")
             for i in range(n):
@@ -110,12 +106,12 @@ def tile_picked_ygjrg_put_p_kernel(tc, x_words, x_scales, w1, var, omega, offs, 
                         out=y_t[:, i],
                         lhsT=x_code[g][:, cols].bitcast(FP8X4),
                         lhsT_scale=x_scale[4 * g :, cols],
-                        rhs=w_code[b][:, g].bitcast(FP8X4),
-                        rhs_scale=w_scale[b][:, g],
+                        rhs=w_code[g][:, b * P : (b + 1) * P].bitcast(FP8X4),
+                        rhs_scale=w_scale[g][:, b * P : (b + 1) * P],
                         start=(g == 0),
                         stop=(g == PASSES - 1),
                     )
-            neg = held.tile([P, n, P], F32, name=f"neg{b}_{lo}", tag=neg_tag, align_bytes=64)
+            neg = held.tile([P, n, P], F32, name=f"neg{b}_{lo}", align_bytes=64)
             neg_sq = held.tile([P, n, P], F32, name=f"neg_sq{b}_{lo}", align_bytes=64)
             sym_sq = held.tile([P, n, P], F32, name=f"sym_sq{b}_{lo}", align_bytes=64)
             nc.scalar.activation(neg[:], y_t[:], ACT.Relu, scale=-ROOT_NEG)
@@ -128,40 +124,31 @@ def tile_picked_ygjrg_put_p_kernel(tc, x_words, x_scales, w1, var, omega, offs, 
                 nc.tensor.matmul(dst, neg_sq[:, i], ident[:], start=False, stop=True, is_transpose=True)
             return acc
 
-        def put_back(b, lo, hi, acc, tag):
-            scaled = held.tile([P, hi - lo], F32, name=f"scaled{b}_{lo}", tag=tag, align_bytes=64)
-            nc.vector.scalar_tensor_tensor(scaled[:], acc[:], KEEP, v0[b][:, lo:hi], ALU.add, ALU.mult)
-            nc.vector.tensor_tensor(var_sb[b][:].indirect(entries(ser_sb, lo, hi)), scaled[:], omega_wide[b][:], ALU.add)
+        def scale(b, lo, hi, acc):
+            nc.vector.scalar_tensor_tensor(scaled[b][:, lo:hi], acc[:], KEEP, v0[:, b, lo:hi], ALU.add, ALU.mult)
 
-        def gather_var(b, tag):
-            v0[b] = held.tile([P, S], F32, name=f"v0_{b}", tag=tag, align_bytes=64)
-            nc.vector.tensor_copy(v0[b][:], var_sb[b][:].indirect(ser_sb[:]))
+        def put_back(b, lo, hi):
+            nc.vector.tensor_tensor(var_sb[b][:].indirect(entries(ser_sb, lo, hi)), scaled[b][:, lo:hi], omega_wide[b][:], ALU.add)
 
-        half = S // 2
+        for q in range(4):
+            rows = slice(32 * q, 32 * q + 4 * PASSES)
+            nc.vector.tensor_copy(scale_tab[rows, :].bitcast(I32), scale_rows[rows, :])
         nc.vector.tensor_copy(x_scale[:], scale_tab[:].indirect(offs_sb[:]))
-        gather_words(0, 0, S)
-        load_var(0)
-        for g in range(PASSES):
-            cast_w(0, g, "w_bf0")
-            quantise_w(0, g, g + 1, "w_code0")
-        load_w(1)
         for b in range(BLOCKS):
-            nc.scalar.copy(omega_wide[b][:], omega_sb[:, b : b + 1].to_broadcast([P, S // 2]))
-        gather_words(1, 0, half)
-        gather_words(1, half, S)
-        load_var(1)
-        acc_a = growth(0, 0, half, "chain")
-        acc_b = growth(0, half, S, "neg_b")
-        gather_var(0, "v0_0")
+            nc.scalar.copy(omega_wide[b][:], omega_sb[:, b : b + 1].to_broadcast([P, (half, S)[b]]))
         for g in range(PASSES):
-            cast_w(1, g, "chain")
-        put_back(0, 0, half, acc_a, "first")
-        quantise_w(1, 0, PASSES, "first")
-        acc_c = growth(1, 0, half, "neg_c")
-        acc_d = growth(1, half, S, "neg_d")
-        put_back(0, half, S, acc_b, "chain")
+            gather_words(g, 0, S)
+        quantise_w(0, 0, N)
+        for b in range(BLOCKS):
+            quantise_w(1, b * P, (b + 1) * P)
+        acc = {(b, lo): growth(b, lo, lo + half) for b in range(BLOCKS) for lo in (0, half)}
+        gather_var(0)
+        gather_var(1)
+        for lo in (0, half):
+            scale(0, lo, lo + half, acc[0, lo])
+            put_back(0, lo, lo + half)
         nc.sync.dma_start(out[0:P, :], var_sb[0][:])
-        gather_var(1, "chain")
-        put_back(1, 0, half, acc_c, "scaled_c")
-        put_back(1, half, S, acc_d, "scaled_d")
+        for lo in (0, half):
+            scale(1, lo, lo + half, acc[1, lo])
+        put_back(1, 0, S)
         nc.sync.dma_start(out[P : 2 * P, :], var_sb[1][:])

@@ -22,10 +22,17 @@ PACK = 4
 K_PASS = P * PACK
 PASSES = K // K_PASS
 BLOCKS = N // P
+QUADRANT = 32
+SCALE_ROWS = 4
 LIST_COL = 16
-ROOT_SYM = 0.9 * math.sqrt(0.08)
+LINE = 4
+HALF = S // 2
+ROOT_BOTH = 0.9 * math.sqrt(0.08)
 ROOT_NEG = 0.9 * math.sqrt(0.12)
 KEEP = 0.8
+
+PIECES = [[(0, P), (P, S)], [(0, HALF), (HALF, S)]]
+BANKS = [[("y0", "sum0"), ("y1", "sum1")], [("sum0", "y0"), ("y1", "sum2")]]
 
 
 def tile_picked_ygjrg_put_p_kernel(tc, x_words, x_scales, w1, var, omega, offs, ser, out):
@@ -33,7 +40,6 @@ def tile_picked_ygjrg_put_p_kernel(tc, x_words, x_scales, w1, var, omega, offs, 
     with ExitStack() as ctx:
         held = ctx.enter_context(tc.tile_pool(name="held", bufs=1))
         psum = ctx.enter_context(tc.psum_pool(name="psum", bufs=1))
-        half = S // 2
 
         offs_sb = held.tile([P, S // LIST_COL], U16, name="offs_sb")
         ser_sb = held.tile([P, S // LIST_COL], U16, name="ser_sb")
@@ -43,46 +49,41 @@ def tile_picked_ygjrg_put_p_kernel(tc, x_words, x_scales, w1, var, omega, offs, 
         w_raw = [held.tile([P, PACK, N], F32, name=f"w_raw{g}", align_bytes=64) for g in range(PASSES)]
         omega_sb = held.tile([P, BLOCKS], F32, name="omega_sb")
         ident = held.tile([P, P], F32, name="ident", align_bytes=64)
-        var_sb = {}
-
-        def load_var(b):
-            var_sb[b] = held.tile([P, U], F32, name=f"var_sb{b}", align_bytes=64)
-            nc.sync.dma_start(var_sb[b][:], var[b * P : (b + 1) * P, :])
-
-        def load_words(g):
-            nc.sync.dma_start(word_tab[g][:].bitcast(I32), x_words[g].rearrange("p n t -> p (n t)").bitcast(I32))
+        var_sb = [held.tile([P, U], F32, name=f"var_sb{b}", align_bytes=64) for b in range(BLOCKS)]
+        quadrant_rows = [slice(QUADRANT * q, QUADRANT * q + SCALE_ROWS * PASSES) for q in range(P // QUADRANT)]
 
         nc.gpsimd.memset(scale_tab[:].bitcast(I32), 0)
         nc.sync.dma_start(offs_sb[:], offs)
-        for q in range(4):
-            nc.sync.dma_start(scale_rows[32 * q : 32 * q + 4 * PASSES, :], x_scales[:, 4 * q : 4 * q + 4, :].bitcast(I32))
+        for q, rows in enumerate(quadrant_rows):
+            nc.sync.dma_start(scale_rows[rows, :], x_scales[:, SCALE_ROWS * q : SCALE_ROWS * (q + 1), :].bitcast(I32))
         with nc.allow_non_contiguous_dma(reason="one constant a row"):
-            nc.sync.dma_start(omega_sb[:], omega.rearrange("(b p) o -> p (b o)", p=P))
-        load_words(0)
-        load_words(1)
+            nc.scalar.dma_start(omega_sb[:], omega.rearrange("(b p) o -> p (b o)", p=P))
+        for g in range(PASSES):
+            nc.sync.dma_start(word_tab[g][:].bitcast(I32), x_words[g].rearrange("p n t -> p (n t)").bitcast(I32))
         for g in range(PASSES):
             nc.sync.dma_start(w_raw[g][:], w1[g * K_PASS : (g + 1) * K_PASS, :].rearrange("(p j) c -> p j c", j=PACK))
         nc.sync.dma_start(ser_sb[:], ser)
-        load_var(0)
-        load_var(1)
+        for b in range(BLOCKS):
+            nc.sync.dma_start(var_sb[b][:], var[b * P : (b + 1) * P, :])
         make_identity(nc, ident[:])
 
-        omega_wide = [held.tile([P, (half, S)[b]], F32, name=f"omega_wide{b}", align_bytes=64) for b in range(BLOCKS)]
+        omega_width = [S - P, S]
+        omega_wide = [held.tile([P, omega_width[b]], F32, name=f"omega_wide{b}", align_bytes=64) for b in range(BLOCKS)]
         x_scale = held.tile([P, S], U8, name="x_scale", align_bytes=64)
         x_code = [held.tile([P, S], U32, name=f"x_code{g}", align_bytes=64) for g in range(PASSES)]
         w_code = [held.tile([P, N], U32, name=f"w_code{g}", align_bytes=64) for g in range(PASSES)]
         w_scale = [held.tile([P, N], U8, name=f"w_scale{g}", align_bytes=64) for g in range(PASSES)]
         w_bf = [held.tile([P, N, PACK], BF16, name=f"w_bf{g}", align_bytes=64) for g in range(PASSES)]
-        v0 = held.tile([P, BLOCKS, S], F32, name="v0", align_bytes=64)
+        v0 = held.tile([P, S + HALF], F32, name="v0", align_bytes=64)
         scaled = [held.tile([P, S], F32, name=f"scaled{b}", align_bytes=64) for b in range(BLOCKS)]
 
         def entries(lst, lo, hi):
             return lst[:, lo // LIST_COL : hi // LIST_COL]
 
-        def quantise_w(g, lo, hi):
-            nc.scalar.copy(
-                w_bf[g][:, lo:hi].rearrange("p (c i) t -> p c t i", i=4),
-                w_raw[g][:, :, lo:hi].rearrange("p t (c i) -> p c t i", i=4),
+        def quantise_w(g, lo, hi, copy):
+            copy(
+                w_bf[g][:, lo:hi].rearrange("p (c i) t -> p c t i", i=LINE),
+                w_raw[g][:, :, lo:hi].rearrange("p t (c i) -> p c t i", i=LINE),
             )
             nc.vector.quantize_mx(
                 out=w_code[g][:, lo:hi].bitcast(FP8X4),
@@ -90,22 +91,21 @@ def tile_picked_ygjrg_put_p_kernel(tc, x_words, x_scales, w1, var, omega, offs, 
                 in_=w_bf[g][:, lo:hi].rearrange("p c t -> p (c t)"),
             )
 
-        def gather_words(g, lo, hi):
-            nc.vector.tensor_copy(x_code[g][:, lo:hi], word_tab[g][:].indirect(entries(offs_sb, lo, hi)))
+        def gather_var(b, lo, hi, at):
+            nc.vector.tensor_copy(v0[:, at : at + hi - lo], var_sb[b][:].indirect(entries(ser_sb, lo, hi)))
 
-        def gather_var(b):
-            nc.vector.tensor_copy(v0[:, b], var_sb[b][:].indirect(ser_sb[:]))
-
-        def growth(b, lo, hi):
+        def squares(b, i):
+            lo, hi = PIECES[b][i]
+            y_bank, sum_bank = BANKS[b][i]
             n = (hi - lo) // P
-            y_t = psum.tile([P, n, P], F32, name=f"y_t{b}_{lo}")
-            for i in range(n):
-                cols = slice(lo + i * P, lo + (i + 1) * P)
+            y_t = psum.tile([P, n, P], F32, name=f"y_t{b}_{lo}", tag=y_bank)
+            for c in range(n):
+                cols = slice(lo + c * P, lo + (c + 1) * P)
                 for g in range(PASSES):
                     nc.tensor.matmul_mx(
-                        out=y_t[:, i],
+                        out=y_t[:, c],
                         lhsT=x_code[g][:, cols].bitcast(FP8X4),
-                        lhsT_scale=x_scale[4 * g :, cols],
+                        lhsT_scale=x_scale[SCALE_ROWS * g :, cols],
                         rhs=w_code[g][:, b * P : (b + 1) * P].bitcast(FP8X4),
                         rhs_scale=w_scale[g][:, b * P : (b + 1) * P],
                         start=(g == 0),
@@ -113,42 +113,47 @@ def tile_picked_ygjrg_put_p_kernel(tc, x_words, x_scales, w1, var, omega, offs, 
                     )
             neg = held.tile([P, n, P], F32, name=f"neg{b}_{lo}", align_bytes=64)
             neg_sq = held.tile([P, n, P], F32, name=f"neg_sq{b}_{lo}", align_bytes=64)
-            sym_sq = held.tile([P, n, P], F32, name=f"sym_sq{b}_{lo}", align_bytes=64)
+            both_sq = held.tile([P, n, P], F32, name=f"both_sq{b}_{lo}", align_bytes=64)
             nc.scalar.activation(neg[:], y_t[:], ACT.Relu, scale=-ROOT_NEG)
-            nc.scalar.activation(sym_sq[:], y_t[:], ACT.Square, scale=ROOT_SYM)
+            nc.scalar.activation(both_sq[:], y_t[:], ACT.Square, scale=ROOT_BOTH)
             nc.scalar.activation(neg_sq[:], neg[:], ACT.Square)
-            acc = psum.tile([P, n * P], F32, name=f"acc{b}_{lo}")
-            for i in range(n):
-                dst = acc[:, i * P : (i + 1) * P]
-                nc.tensor.matmul(dst, sym_sq[:, i], ident[:], start=True, stop=False, is_transpose=True)
-                nc.tensor.matmul(dst, neg_sq[:, i], ident[:], start=False, stop=True, is_transpose=True)
-            return acc
+            total = psum.tile([P, n * P], F32, name=f"total{b}_{lo}", tag=sum_bank)
+            for c in range(n):
+                dst = total[:, c * P : (c + 1) * P]
+                nc.tensor.matmul(dst, both_sq[:, c], ident[:], start=True, stop=False, is_transpose=True)
+                nc.tensor.matmul(dst, neg_sq[:, c], ident[:], start=False, stop=True, is_transpose=True)
+            return total
 
-        def scale(b, lo, hi, acc):
-            nc.vector.scalar_tensor_tensor(scaled[b][:, lo:hi], acc[:], KEEP, v0[:, b, lo:hi], ALU.add, ALU.mult)
+        def scale_var(b, i, total, at):
+            lo, hi = PIECES[b][i]
+            nc.vector.scalar_tensor_tensor(scaled[b][:, lo:hi], total[:], KEEP, v0[:, at : at + hi - lo], ALU.add, ALU.mult)
 
         def put_back(b, lo, hi):
-            nc.vector.tensor_tensor(var_sb[b][:].indirect(entries(ser_sb, lo, hi)), scaled[b][:, lo:hi], omega_wide[b][:], ALU.add)
+            nc.vector.tensor_tensor(var_sb[b][:].indirect(entries(ser_sb, lo, hi)), scaled[b][:, lo:hi], omega_wide[b][:, : hi - lo], ALU.add)
 
-        for q in range(4):
-            rows = slice(32 * q, 32 * q + 4 * PASSES)
+        for rows in quadrant_rows:
             nc.vector.tensor_copy(scale_tab[rows, :].bitcast(I32), scale_rows[rows, :])
         nc.vector.tensor_copy(x_scale[:], scale_tab[:].indirect(offs_sb[:]))
         for b in range(BLOCKS):
-            nc.scalar.copy(omega_wide[b][:], omega_sb[:, b : b + 1].to_broadcast([P, (half, S)[b]]))
+            nc.scalar.copy(omega_wide[b][:], omega_sb[:, b : b + 1].to_broadcast([P, omega_width[b]]))
         for g in range(PASSES):
-            gather_words(g, 0, S)
-        quantise_w(0, 0, N)
-        for b in range(BLOCKS):
-            quantise_w(1, b * P, (b + 1) * P)
-        acc = {(b, lo): growth(b, lo, lo + half) for b in range(BLOCKS) for lo in (0, half)}
-        gather_var(0)
-        gather_var(1)
-        for lo in (0, half):
-            scale(0, lo, lo + half, acc[0, lo])
-            put_back(0, lo, lo + half)
+            nc.vector.tensor_copy(x_code[g][:], word_tab[g][:].indirect(offs_sb[:]))
+
+        quantise_w(0, 0, N, nc.scalar.copy)
+        quantise_w(1, 0, P, nc.vector.tensor_copy)
+        quantise_w(1, P, N, nc.scalar.copy)
+
+        totals0 = [squares(0, i) for i in range(len(PIECES[0]))]
+        gather_var(0, 0, S, 0)
+        gather_var(1, HALF, S, S)
+        totals1 = []
+        for i, (lo, hi) in enumerate(PIECES[0]):
+            scale_var(0, i, totals0[i], lo)
+            totals1.append(squares(1, i))
+            gather_var(1, i * P, (i + 1) * P, i * P)
+            put_back(0, lo, hi)
         nc.sync.dma_start(out[0:P, :], var_sb[0][:])
-        for lo in (0, half):
-            scale(1, lo, lo + half, acc[1, lo])
+        scale_var(1, 0, totals1[0], 0)
+        scale_var(1, 1, totals1[1], S)
         put_back(1, 0, S)
-        nc.sync.dma_start(out[P : 2 * P, :], var_sb[1][:])
+        nc.sync.dma_start(out[P:N, :], var_sb[1][:])

import math
from contextlib import ExitStack

import concourse.mybir as mybir
from concourse.masks import make_identity

K, T, S, N, U = 1024, 1024, 512, 256, 1024
FLOPS = 2 * K * N * S

F32 = mybir.dt.float32
BF16 = mybir.dt.bfloat16
I32 = mybir.dt.int32
U32 = mybir.dt.uint32
U16 = mybir.dt.uint16
U8 = mybir.dt.uint8
FP8X4 = mybir.dt.float8_e4m3fn_x4
ACT = mybir.ActivationFunctionType
ALU = mybir.AluOpType

P = 128
PACK = 4
K_PASS = P * PACK
PASSES = K // K_PASS
BLOCKS = N // P
QUADRANT = 32
SCALE_ROWS = 4
LIST_COL = 16
LINE = 4
HALF = S // 2
ROOT_BOTH = 0.9 * math.sqrt(0.08)
ROOT_NEG = 0.9 * math.sqrt(0.12)
KEEP = 0.8

PIECES = [[(0, P), (P, S)], [(0, HALF), (HALF, S)]]
BANKS = [[("y0", "sum0"), ("y1", "sum1")], [("sum0", "y0"), ("y1", "sum2")]]


def tile_picked_ygjrg_put_p_kernel(tc, x_words, x_scales, w1, var, omega, offs, ser, out):
    nc = tc.nc
    with ExitStack() as ctx:
        held = ctx.enter_context(tc.tile_pool(name="held", bufs=1))
        psum = ctx.enter_context(tc.psum_pool(name="psum", bufs=1))

        offs_sb = held.tile([P, S // LIST_COL], U16, name="offs_sb")
        ser_sb = held.tile([P, S // LIST_COL], U16, name="ser_sb")
        scale_tab = held.tile([P, T], U8, name="scale_tab", align_bytes=64)
        scale_rows = held.tile([P, T // 4], I32, name="scale_rows", align_bytes=64)
        word_tab = [held.tile([P, T], U32, name=f"word_tab{g}", align_bytes=64) for g in range(PASSES)]
        w_raw = [held.tile([P, PACK, N], F32, name=f"w_raw{g}", align_bytes=64) for g in range(PASSES)]
        omega_sb = held.tile([P, BLOCKS], F32, name="omega_sb")
        ident = held.tile([P, P], F32, name="ident", align_bytes=64)
        var_sb = [held.tile([P, U], F32, name=f"var_sb{b}", align_bytes=64) for b in range(BLOCKS)]
        quadrant_rows = [slice(QUADRANT * q, QUADRANT * q + SCALE_ROWS * PASSES) for q in range(P // QUADRANT)]

        nc.gpsimd.memset(scale_tab[:].bitcast(I32), 0)
        nc.sync.dma_start(offs_sb[:], offs)
        for q, rows in enumerate(quadrant_rows):
            nc.sync.dma_start(scale_rows[rows, :], x_scales[:, SCALE_ROWS * q : SCALE_ROWS * (q + 1), :].bitcast(I32))
        with nc.allow_non_contiguous_dma(reason="one constant a row"):
            nc.scalar.dma_start(omega_sb[:], omega.rearrange("(b p) o -> p (b o)", p=P))
        for g in range(PASSES):
            nc.sync.dma_start(word_tab[g][:].bitcast(I32), x_words[g].rearrange("p n t -> p (n t)").bitcast(I32))
        for g in range(PASSES):
            nc.sync.dma_start(w_raw[g][:], w1[g * K_PASS : (g + 1) * K_PASS, :].rearrange("(p j) c -> p j c", j=PACK))
        nc.sync.dma_start(ser_sb[:], ser)
        for b in range(BLOCKS):
            nc.sync.dma_start(var_sb[b][:], var[b * P : (b + 1) * P, :])
        make_identity(nc, ident[:])

        omega_width = [S - P, S]
        omega_wide = [held.tile([P, omega_width[b]], F32, name=f"omega_wide{b}", align_bytes=64) for b in range(BLOCKS)]
        x_scale = held.tile([P, S], U8, name="x_scale", align_bytes=64)
        x_code = [held.tile([P, S], U32, name=f"x_code{g}", align_bytes=64) for g in range(PASSES)]
        w_code = [held.tile([P, N], U32, name=f"w_code{g}", align_bytes=64) for g in range(PASSES)]
        w_scale = [held.tile([P, N], U8, name=f"w_scale{g}", align_bytes=64) for g in range(PASSES)]
        w_bf = [held.tile([P, N, PACK], BF16, name=f"w_bf{g}", align_bytes=64) for g in range(PASSES)]
        v0 = held.tile([P, S + HALF], F32, name="v0", align_bytes=64)
        scaled = [held.tile([P, S], F32, name=f"scaled{b}", align_bytes=64) for b in range(BLOCKS)]

        def entries(lst, lo, hi):
            return lst[:, lo // LIST_COL : hi // LIST_COL]

        def quantise_w(g, lo, hi, copy):
            copy(
                w_bf[g][:, lo:hi].rearrange("p (c i) t -> p c t i", i=LINE),
                w_raw[g][:, :, lo:hi].rearrange("p t (c i) -> p c t i", i=LINE),
            )
            nc.vector.quantize_mx(
                out=w_code[g][:, lo:hi].bitcast(FP8X4),
                scales=w_scale[g][:, lo:hi],
                in_=w_bf[g][:, lo:hi].rearrange("p c t -> p (c t)"),
            )

        def gather_var(b, lo, hi, at):
            nc.vector.tensor_copy(v0[:, at : at + hi - lo], var_sb[b][:].indirect(entries(ser_sb, lo, hi)))

        def squares(b, i):
            lo, hi = PIECES[b][i]
            y_bank, sum_bank = BANKS[b][i]
            n = (hi - lo) // P
            y_t = psum.tile([P, n, P], F32, name=f"y_t{b}_{lo}", tag=y_bank)
            for c in range(n):
                cols = slice(lo + c * P, lo + (c + 1) * P)
                for g in range(PASSES):
                    nc.tensor.matmul_mx(
                        out=y_t[:, c],
                        lhsT=x_code[g][:, cols].bitcast(FP8X4),
                        lhsT_scale=x_scale[SCALE_ROWS * g :, cols],
                        rhs=w_code[g][:, b * P : (b + 1) * P].bitcast(FP8X4),
                        rhs_scale=w_scale[g][:, b * P : (b + 1) * P],
                        start=(g == 0),
                        stop=(g == PASSES - 1),
                    )
            neg = held.tile([P, n, P], F32, name=f"neg{b}_{lo}", align_bytes=64)
            neg_sq = held.tile([P, n, P], F32, name=f"neg_sq{b}_{lo}", align_bytes=64)
            both_sq = held.tile([P, n, P], F32, name=f"both_sq{b}_{lo}", align_bytes=64)
            nc.scalar.activation(neg[:], y_t[:], ACT.Relu, scale=-ROOT_NEG)
            nc.scalar.activation(both_sq[:], y_t[:], ACT.Square, scale=ROOT_BOTH)
            nc.scalar.activation(neg_sq[:], neg[:], ACT.Square)
            total = psum.tile([P, n * P], F32, name=f"total{b}_{lo}", tag=sum_bank)
            for c in range(n):
                dst = total[:, c * P : (c + 1) * P]
                nc.tensor.matmul(dst, both_sq[:, c], ident[:], start=True, stop=False, is_transpose=True)
                nc.tensor.matmul(dst, neg_sq[:, c], ident[:], start=False, stop=True, is_transpose=True)
            return total

        def scale_var(b, i, total, at):
            lo, hi = PIECES[b][i]
            nc.vector.scalar_tensor_tensor(scaled[b][:, lo:hi], total[:], KEEP, v0[:, at : at + hi - lo], ALU.add, ALU.mult)

        def put_back(b, lo, hi):
            nc.vector.tensor_tensor(var_sb[b][:].indirect(entries(ser_sb, lo, hi)), scaled[b][:, lo:hi], omega_wide[b][:, : hi - lo], ALU.add)

        for rows in quadrant_rows:
            nc.vector.tensor_copy(scale_tab[rows, :].bitcast(I32), scale_rows[rows, :])
        nc.vector.tensor_copy(x_scale[:], scale_tab[:].indirect(offs_sb[:]))
        for b in range(BLOCKS):
            nc.scalar.copy(omega_wide[b][:], omega_sb[:, b : b + 1].to_broadcast([P, omega_width[b]]))
        for g in range(PASSES):
            nc.vector.tensor_copy(x_code[g][:], word_tab[g][:].indirect(offs_sb[:]))

        quantise_w(0, 0, N, nc.scalar.copy)
        quantise_w(1, 0, P, nc.vector.tensor_copy)
        quantise_w(1, P, N, nc.scalar.copy)

        totals0 = [squares(0, i) for i in range(len(PIECES[0]))]
        gather_var(0, 0, S, 0)
        gather_var(1, HALF, S, S)
        totals1 = []
        for i, (lo, hi) in enumerate(PIECES[0]):
            scale_var(0, i, totals0[i], lo)
            totals1.append(squares(1, i))
            gather_var(1, i * P, (i + 1) * P, i * P)
            put_back(0, lo, hi)
        nc.sync.dma_start(out[0:P, :], var_sb[0][:])
        scale_var(1, 0, totals1[0], 0)
        scale_var(1, 1, totals1[1], S)
        put_back(1, 0, S)
        nc.sync.dma_start(out[P:N, :], var_sb[1][:])
